import numpy as np
import ml_dtypes


def mxq(x, axis, fmt="e4m3"):
    dtype, down = {"e4m3": (ml_dtypes.float8_e4m3fn, 7), "e5m2": (ml_dtypes.float8_e5m2, 14)}[fmt]
    v = np.moveaxis(np.asarray(x, np.float32).astype(ml_dtypes.bfloat16).astype(np.float64), axis, -1)
    blocks = v.reshape(v.shape[:-1] + (-1, 32))
    amax = np.abs(blocks).max(-1, keepdims=True)
    byte = np.maximum(np.where(amax > 0, np.frexp(amax)[1] - 1 + 127, 0) - down, 1)
    scale = np.exp2(byte - 127.0)
    codes = (blocks / scale).astype(np.float32).astype(dtype).astype(np.float64)
    return np.moveaxis((codes * scale).reshape(v.shape), -1, axis)


WIDE = False


def mx_kscale(k):
    if not WIDE:
        return np.ones(k)
    levels = np.array([18, -18])
    if k % 512:
        return np.exp2(np.random.permutation(np.resize(levels, k // 32))).repeat(32)
    a = np.empty((k // 512, 16))
    for p in range(k // 512):
        a[p, :8] = np.random.permutation(np.resize(levels, 8))
        for g in range(8):
            far = levels[np.abs(levels - a[p, g]) >= 10]
            a[p, g + 8] = far[np.random.randint(len(far))]
    return np.exp2(a.ravel()).repeat(32)


def f64(x):
    return np.asarray(x).astype(np.float64)


def striped(idx):
    return np.tile(np.asarray(idx).reshape(-1, 16).T, (8, 1)).astype(np.uint16)


def unstriped(offs):
    return offs[:16].T.reshape(-1).astype(np.int64)


def setup_inputs():
    n = np.random.standard_normal
    uni = np.random.uniform
    order = np.random.permutation(2048)
    idx = order[:512]
    win = order[512:1024]
    f_d = mx_kscale(512)
    f_r = mx_kscale(512)
    return {
        "qT": (0.5 * n((512, 512)) * f_d[:, None] * f_r[None, :]).astype(np.float32),
        "kT": (n((512, 2048)) / np.sqrt(512) / f_d[:, None]).astype(np.float32),
        "dp": (n((512, 512))).astype(np.float32),
        "dq": (n((512, 512))).astype(np.float32),
        "us": (uni(0.75, 1.3, (512, 1)) / f_r[:, None]).astype(np.float32),
        "ts": np.tile(uni(0.75, 1.3, 2048), (128, 1)).astype(np.float32),
        "wt": (uni(0.75, 1.3, (512, 1))).astype(np.float32),
        "offs": striped(idx),
        "woffs": striped(win),
    }


def reference(qT, kT, dp, dq, us, ts, wt, offs, woffs):
    idx = unstriped(offs)
    win = unstriped(woffs)
    kT_i = f64(kT)[:, idx]
    kT_j = f64(kT)[:, win]
    ts_i = f64(ts)[:1][:, idx]
    ts_j = f64(ts)[:1][:, win]
    q_qT = mxq(f64(qT), 0, "e4m3")
    a = q_qT.T @ mxq(kT_i, 0, "e4m3")
    b = q_qT.T @ mxq(kT_j, 0, "e4m3")
    z = f64(us) * ts_i * a
    y = f64(us) * ts_j * b
    m1 = (z).max(-1, keepdims=True)
    m2 = (y).max(-1, keepdims=True)
    m = np.maximum(m1, m2)
    e = np.exp(z - m)
    f = np.exp(y - m)
    t1 = (e).sum(-1, keepdims=True)
    t2 = (f).sum(-1, keepdims=True)
    inv = 1.0 / (t1 + t2)
    s1 = (e * f64(dp)).sum(-1, keepdims=True)
    s2 = (f * f64(dq)).sum(-1, keepdims=True)
    c = inv * (s1 + s2)
    g = f64(wt) * f64(us) * ts_i * inv * e * (f64(dp) - c)
    h = f64(wt) * f64(us) * ts_j * inv * f * (f64(dq) - c)
    q_qT_2 = mxq(f64(qT), 1, "e4m3")
    d1 = q_qT_2 @ mxq(g, 0, "e5m2")
    d2 = q_qT_2 @ mxq(h, 0, "e5m2")
    k1 = np.zeros((512, 2048))
    k1[:, idx] = d1
    k2 = np.zeros((512, 2048))
    k2[:, win] = d2
    out = k1 + k2
    return out

@@ -1,0 +1,239 @@
+from contextlib import ExitStack
+
+import concourse.mybir as mybir
+from concourse.masks import make_identity
+
+F32 = mybir.dt.float32
+BF16 = mybir.dt.bfloat16
+U32 = mybir.dt.uint32
+U16 = mybir.dt.uint16
+U8 = mybir.dt.uint8
+E4M3 = mybir.dt.float8_e4m3fn_x4
+E5M2 = mybir.dt.float8_e5m2_x4
+ALU = mybir.AluOpType
+ACT = mybir.ActivationFunctionType
+AXIS = mybir.AxisListType
+
+P = 128
+PACK = 4
+D = 512
+R = 512
+SLOTS = 512
+TOKENS = 2048
+FLOPS = 4 * 2 * D * R * SLOTS
+
+
+def tile_attend_gjoint_kk_kernel(tc, qT, kT, dp, dq, us, ts, wt, offs, woffs, out):
+    nc = tc.nc
+    with ExitStack() as ctx:
+        sb = ctx.enter_context(tc.tile_pool(name="sb", bufs=1))
+        ps = ctx.enter_context(tc.psum_pool(name="ps", bufs=1))
+
+        def sbuf(name, shape, dtype, tag=None):
+            return sb.tile(shape, dtype, name=name, tag=tag or name, align_bytes=64)
+
+        def bank(n, name, shape, dtype=F32):
+            return ps.tile(shape, dtype, name=name, tag="bank%d" % n)
+
+        def quantise(name, src, fmt):
+            codes = sbuf(name + "_codes", [P, 512], U32)
+            scales = sbuf(name + "_scales", [P, 512], U8)
+            nc.vector.quantize_mx(out=codes[:].bitcast(fmt), scales=scales[:], in_=src)
+            return codes, scales
+
+        def mx(dst, lhs, cols, rhs, rhs_fmt):
+            nc.tensor.matmul_mx(out=dst, lhsT=lhs[0][:, cols].bitcast(E4M3), lhsT_scale=lhs[1][:, cols],
+                                rhs=rhs[0][:].bitcast(rhs_fmt), rhs_scale=rhs[1][:], start=True, stop=True)
+
+        def blk(b):
+            return slice(b * P, (b + 1) * P)
+
+        lists = [sbuf("offs_sb", [P, SLOTS // 16], U16), sbuf("woffs_sb", [P, SLOTS // 16], U16)]
+        nc.sync.dma_start(lists[0][:], offs)
+        nc.sync.dma_start(lists[1][:], woffs)
+        ts_win = sbuf("ts_win", [P, TOKENS], F32)
+        nc.sync.dma_start(ts_win[P - 1:P, :], ts[P - 1:P, :])
+        k_rows = kT.rearrange("(p j) c -> p j c", j=PACK)
+        planes = [sbuf("k_plane%d" % j, [P, TOKENS], F32) for j in range(PACK)]
+        q_raw = sbuf("q_raw", [P, PACK, R], F32)
+        nc.sync.dma_start(planes[0][:], k_rows[:, 0, :])
+        nc.sync.dma_start(q_raw[:], qT.rearrange("(p j) r -> p j r", j=PACK))
+        for j in range(1, PACK):
+            nc.sync.dma_start(planes[j][:], k_rows[:, j, :])
+        us_sb = sbuf("us_sb", [P, PACK], F32)
+        wt_sb = sbuf("wt_sb", [P, PACK], F32)
+        nc.sync.dma_start(us_sb[:], us.rearrange("(p t) o -> p (t o)", t=PACK))
+        nc.sync.dma_start(wt_sb[:], wt.rearrange("(p t) o -> p (t o)", t=PACK))
+        dpq = sbuf("dpq", [P, 2, PACK, SLOTS], F32)
+        for half in range(2):
+            for l, grad in enumerate((dp, dq)):
+                rows = slice(2 * half, 2 * half + 2)
+                nc.sync.dma_start(dpq[:, l, rows, :], grad.rearrange("(p t) c -> p t c", t=PACK)[:, rows, :])
+
+        ident = sbuf("ident", [P, P], F32)
+        make_identity(nc, ident[:])
+        ident_bf = sbuf("ident_bf", [P, P], BF16)
+        make_identity(nc, ident_bf[:])
+
+        nc.vector.memset(ts_win[0:P - 1, :], 0.0)
+        windows = [sbuf("window%d" % j, [P, TOKENS], F32) for j in range(2)]
+        for j in range(2):
+            nc.vector.memset(windows[j][:], 0.0)
+
+        ts_g = sbuf("ts_g", [P, 2, SLOTS], F32)
+        ts_col = []
+        for l in range(2):
+            nc.vector.tensor_copy(ts_g[:, l, :], ts_win[:].indirect(lists[l][:]))
+            turned = bank(l, "ts_turned%d" % l, [P, PACK, P])
+            for b in range(PACK):
+                nc.tensor.transpose(turned[:, b, :], ts_g[:, l, blk(b)], ident[:])
+            col = sbuf("ts_col%d" % l, [P, PACK], F32)
+            nc.scalar.activation(col[:], turned[:, :, P - 1], ACT.Copy)
+            ts_col.append(col)
+        spread = bank(2, "ts_spread", [P, SLOTS])
+        for b in range(PACK):
+            nc.tensor.transpose(spread[:, blk(b)], ts_col[1][:, b:b + 1].to_broadcast([P, P]), ident[:])
+        ts_row = sbuf("ts_row", [P, SLOTS], F32)
+        nc.scalar.copy(ts_row[:], spread[:])
+
+        k_g = [sbuf("k_g%d" % l, [P, PACK, SLOTS], BF16) for l in range(2)]
+
+        def gather_plane(j):
+            for l in range(2):
+                nc.vector.tensor_copy(k_g[l][:, j, :], planes[j][:].indirect(lists[l][:]))
+
+        gather_plane(0)
+
+        q_il = sbuf("q_il", [P, PACK, P, PACK], BF16)
+        nc.scalar.copy(q_il[:].rearrange("p t s j -> p s t j"), q_raw[:].rearrange("p j (s t) -> p s t j", t=PACK))
+        q_d = quantise("q_d", q_il[:].rearrange("p t s j -> p (t s j)"), E4M3)
+
+        for j in range(1, PACK):
+            gather_plane(j)
+
+        q2_il = sbuf("q2_il", [P, PACK, P, PACK], BF16)
+        for j in range(PACK):
+            turned = bank(4 + j, "q_turned%d" % j, [P, PACK, P], BF16)
+            for t in range(PACK):
+                nc.tensor.transpose(turned[:, t, :], q_il[:, t, :, j], ident_bf[:])
+            nc.scalar.copy(q2_il[:, j, :, :], turned[:].rearrange("s t m -> s m t"))
+        q_r = quantise("q_r", q2_il[:].rearrange("s j m t -> s (j m t)"), E4M3)
+
+        neg_us = sbuf("neg_us", [P, PACK], F32)
+        nc.vector.tensor_scalar(neg_us[:], us_sb[:], -1.0, None, ALU.mult)
+        wt_us = sbuf("wt_us", [P, PACK], F32)
+        nc.vector.tensor_tensor(wt_us[:], us_sb[:], wt_sb[:], ALU.mult)
+
+        k_q = []
+        for l in range(2):
+            k_il = sbuf("k_il%d" % l, [P, SLOTS, PACK], BF16)
+            dst = k_il[:].rearrange("p (c i) j -> p c j i", i=4)
+            src = k_g[l][:].rearrange("p j (c i) -> p c j i", i=4)
+            if l == 0:
+                nc.scalar.copy(dst, src)
+            else:
+                nc.vector.tensor_copy(dst, src)
+            k_q.append(quantise("k_q%d" % l, k_il[:].rearrange("p c j -> p (c j)"), E4M3))
+
+        z_turned = []
+        for b in range(PACK):
+            acc = bank(b % 2, "a_turned%d" % b, [P, R])
+            mx(acc[:], k_q[0], blk(b), q_d, E4M3)
+            zt = sbuf("z_turned%d" % b, [P, R], F32)
+            nc.scalar.activation(zt[:], acc[:], ACT.Copy, scale=ts_col[0][:, b:b + 1])
+            z_turned.append(zt)
+        neg_z = [sbuf("neg_z%d" % t, [P, 2, SLOTS], F32) for t in range(PACK)]
+        stat = [sbuf("stat%d" % t, [P, 8], F32) for t in range(PACK)]
+        for t in range(PACK):
+            acc = bank(2 + t % 2, "b%d" % t, [P, SLOTS])
+            mx(acc[:], q_d, blk(t), k_q[1], E4M3)
+            nc.vector.scalar_tensor_tensor(neg_z[t][:, 1, :], acc[:], neg_us[:, t:t + 1], ts_row[:], ALU.mult, ALU.mult)
+            nc.vector.tensor_reduce(stat[t][:, 0:1], neg_z[t][:, 1, :], AXIS.X, ALU.min)
+        z_back = [bank(4 + t, "z_back%d" % t, [P, SLOTS]) for t in range(PACK)]
+        for t in range(PACK):
+            for b in range(PACK):
+                nc.tensor.transpose(z_back[t][:, blk(b)], z_turned[b][:, blk(t)], ident[:])
+
+        windows.append(sbuf("window2", [P, TOKENS], F32, tag="k_il1"))
+        windows.append(sbuf("window3", [P, TOKENS], F32, tag="z_turned0"))
+        for j in range(2, 4):
+            nc.gpsimd.memset(windows[j][:], 0.0)
+
+        v_turned = [bank(b, "v0_turned%d" % b, [P, PACK, P]) for b in range(PACK)]
+        e_all, u_all, ce_all = [], [], []
+
+        def turn_and_add(banks, l, t):
+            for b in range(PACK):
+                nc.tensor.matmul(banks[b][:, t, :], u_all[t][:, l, blk(b)], ident[:], start=True, stop=False,
+                                 is_transpose=True)
+            for b in range(PACK):
+                nc.tensor.matmul(banks[b][:, t, :], ce_all[t][:, l, blk(b)], ident[:], start=False, stop=True,
+                                 is_transpose=True)
+
+        def centre(l, t):
+            nc.scalar.activation(ce_all[t][:, l, :], e_all[t][:, l, :], ACT.Copy, scale=stat[t][:, 6:7])
+
+        for t in range(PACK):
+            st = stat[t]
+            nc.vector.tensor_scalar(neg_z[t][:, 0, :], z_back[t][:], neg_us[:, t:t + 1], st[:, 0:1], ALU.mult, ALU.min,
+                                    accum_out=st[:, 1:2])
+            e = sbuf("e%d" % t, [P, 2, SLOTS], F32)
+            nc.scalar.activation(e[:], neg_z[t][:], ACT.Exp, bias=st[:, 1:2], scale=-1.0, accum_out=st[:, 2:3])
+            nc.vector.reciprocal(st[:, 3:4], st[:, 2:3])
+            nc.vector.tensor_scalar(st[:, 4:5], st[:, 3:4], wt_us[:, t:t + 1], None, ALU.mult)
+            u = sbuf("u%d" % t, [P, 2, SLOTS], F32, tag="k_plane%d" % t)
+            nc.vector.scalar_tensor_tensor(u[:], e[:], st[:, 4:5], dpq[:, :, t, :], ALU.mult, ALU.mult,
+                                           accum_out=st[:, 5:6])
+            nc.vector.tensor_scalar(st[:, 6:7], st[:, 5:6], st[:, 3:4], -1.0, ALU.mult, ALU.mult)
+            ce = sbuf("ce%d" % t, [P, 2, SLOTS], F32, tag="neg_z%d" % t)
+            e_all.append(e)
+            u_all.append(u)
+            ce_all.append(ce)
+            centre(0, t)
+            turn_and_add(v_turned, 0, t)
+
+        def finish(l, banks):
+            g_il = sbuf("g_il%d" % l, [P, SLOTS, PACK], BF16)
+            g_words = g_il[:].rearrange("s c t -> s (c t)").bitcast(F32).rearrange("s (b n u) -> s b n u", b=PACK, u=2)
+            for h in range(2):
+                on_vector = l == 0 and h == 1
+                back = bank(4 + h, "g_back%d_%d" % (l, h), [P, 2, 2, P])
+                for bb in range(2):
+                    b = 2 * h + bb
+                    g_t = sbuf("g_turned%d_%d" % (l, b), [P, 2, P, 2], BF16)
+                    src = banks[b][:].rearrange("n (u e) s -> n u s e", e=2)
+                    if on_vector:
+                        nc.vector.tensor_scalar(g_t[:], src, ts_col[l][:, b:b + 1], None, ALU.mult)
+                    else:
+                        nc.scalar.activation(g_t[:], src, ACT.Copy, scale=ts_col[l][:, b:b + 1])
+                    words = g_t[:].rearrange("n u s e -> n (u s e)").bitcast(F32)
+                    for u in range(2):
+                        nc.tensor.transpose(back[:, bb, u, :], words[:, blk(u)], ident[:])
+                src = back[:].rearrange("s b u n -> s b n u")
+                if on_vector:
+                    nc.vector.tensor_copy(g_words[:, 2 * h:2 * h + 2], src)
+                else:
+                    nc.scalar.copy(g_words[:, 2 * h:2 * h + 2], src)
+            return quantise("g_q%d" % l, g_il[:].rearrange("s c t -> s (c t)"), E5M2)
+
+        out_rows = out.rearrange("(m j) c -> m j c", j=PACK)
+
+        def place(l, j, g_q, tag=None):
+            acc = bank(6 + j % 2, "d%d_%d" % (l, j), [P, SLOTS])
+            mx(acc[:], q_r, blk(j), g_q, E5M2)
+            d_sb = sbuf("d_sb%d_%d" % (l, j), [P, SLOTS], F32, tag=tag)
+            nc.scalar.copy(d_sb[:], acc[:])
+            nc.vector.tensor_copy(windows[j][:].indirect(lists[l][:]), d_sb[:])
+
+        g_q0 = finish(0, v_turned)
+        for j in range(PACK - 1):
+            place(0, j, g_q0)
+        v_turned = [bank(b, "v1_turned%d" % b, [P, PACK, P]) for b in range(PACK)]
+        for t in range(PACK):
+            centre(1, t)
+            turn_and_add(v_turned, 1, t)
+        g_q1 = finish(1, v_turned)
+        place(0, PACK - 1, g_q0, tag="g_il1")
+        for j in range(PACK):
+            place(1, j, g_q1)
+            nc.sync.dma_start(out_rows[:, j, :], windows[j][:])

@@ -20,6 +20,7 @@ D = 512
 R = 512
 SLOTS = 512
 TOKENS = 2048
+Q_SPLIT = 80
 FLOPS = 4 * 2 * D * R * SLOTS
 
 
@@ -35,8 +36,8 @@ def tile_attend_gjoint_kk_kernel(tc, qT, kT, dp, dq, us, ts, wt, offs, woffs, ou
         def bank(n, name, shape, dtype=F32):
             return ps.tile(shape, dtype, name=name, tag="bank%d" % n)
 
-        def quantise(name, src, fmt):
-            codes = sbuf(name + "_codes", [P, 512], U32)
+        def quantise(name, src, fmt, tag=None):
+            codes = sbuf(name + "_codes", [P, 512], U32, tag=tag)
             scales = sbuf(name + "_scales", [P, 512], U8)
             nc.vector.quantize_mx(out=codes[:].bitcast(fmt), scales=scales[:], in_=src)
             return codes, scales
@@ -70,15 +71,12 @@ def tile_attend_gjoint_kk_kernel(tc, qT, kT, dp, dq, us, ts, wt, offs, woffs, ou
                 rows = slice(2 * half, 2 * half + 2)
                 nc.sync.dma_start(dpq[:, l, rows, :], grad.rearrange("(p t) c -> p t c", t=PACK)[:, rows, :])
 
+        nc.gpsimd.memset(ts_win[0:P - 1, :], 0.0)
         ident = sbuf("ident", [P, P], F32)
         make_identity(nc, ident[:])
         ident_bf = sbuf("ident_bf", [P, P], BF16)
         make_identity(nc, ident_bf[:])
 
-        nc.vector.memset(ts_win[0:P - 1, :], 0.0)
-        windows = [sbuf("window%d" % j, [P, TOKENS], F32) for j in range(2)]
-        for j in range(2):
-            nc.vector.memset(windows[j][:], 0.0)
 
         ts_g = sbuf("ts_g", [P, 2, SLOTS], F32)
         ts_col = []
@@ -105,7 +103,10 @@ def tile_attend_gjoint_kk_kernel(tc, qT, kT, dp, dq, us, ts, wt, offs, woffs, ou
         gather_plane(0)
 
         q_il = sbuf("q_il", [P, PACK, P, PACK], BF16)
-        nc.scalar.copy(q_il[:].rearrange("p t s j -> p s t j"), q_raw[:].rearrange("p j (s t) -> p s t j", t=PACK))
+        dst = q_il[:].rearrange("p t s j -> p s t j")
+        src = q_raw[:].rearrange("p j (s t) -> p s t j", t=PACK)
+        nc.vector.tensor_copy(dst[:, :Q_SPLIT], src[:, :Q_SPLIT])
+        nc.scalar.copy(dst[:, Q_SPLIT:], src[:, Q_SPLIT:])
         q_d = quantise("q_d", q_il[:].rearrange("p t s j -> p (t s j)"), E4M3)
 
         for j in range(1, PACK):
@@ -117,12 +118,12 @@ def tile_attend_gjoint_kk_kernel(tc, qT, kT, dp, dq, us, ts, wt, offs, woffs, ou
             for t in range(PACK):
                 nc.tensor.transpose(turned[:, t, :], q_il[:, t, :, j], ident_bf[:])
             nc.scalar.copy(q2_il[:, j, :, :], turned[:].rearrange("s t m -> s m t"))
-        q_r = quantise("q_r", q2_il[:].rearrange("s j m t -> s (j m t)"), E4M3)
 
         neg_us = sbuf("neg_us", [P, PACK], F32)
         nc.vector.tensor_scalar(neg_us[:], us_sb[:], -1.0, None, ALU.mult)
-        wt_us = sbuf("wt_us", [P, PACK], F32)
-        nc.vector.tensor_tensor(wt_us[:], us_sb[:], wt_sb[:], ALU.mult)
+        factors = sbuf("factors", [P, PACK, 2], F32)
+        nc.vector.memset(factors[:, :, 1], -1.0)
+        nc.vector.tensor_tensor(factors[:, :, 0], us_sb[:], wt_sb[:], ALU.mult)
 
         k_q = []
         for l in range(2):
@@ -144,22 +145,25 @@ def tile_attend_gjoint_kk_kernel(tc, qT, kT, dp, dq, us, ts, wt, offs, woffs, ou
             z_turned.append(zt)
         neg_z = [sbuf("neg_z%d" % t, [P, 2, SLOTS], F32) for t in range(PACK)]
         stat = [sbuf("stat%d" % t, [P, 8], F32) for t in range(PACK)]
-        for t in range(PACK):
+
+        def window_scores(t):
             acc = bank(2 + t % 2, "b%d" % t, [P, SLOTS])
             mx(acc[:], q_d, blk(t), k_q[1], E4M3)
             nc.vector.scalar_tensor_tensor(neg_z[t][:, 1, :], acc[:], neg_us[:, t:t + 1], ts_row[:], ALU.mult, ALU.mult)
             nc.vector.tensor_reduce(stat[t][:, 0:1], neg_z[t][:, 1, :], AXIS.X, ALU.min)
+
+        for t in range(PACK):
+            window_scores(t)
         z_back = [bank(4 + t, "z_back%d" % t, [P, SLOTS]) for t in range(PACK)]
         for t in range(PACK):
             for b in range(PACK):
                 nc.tensor.transpose(z_back[t][:, blk(b)], z_turned[b][:, blk(t)], ident[:])
 
-        windows.append(sbuf("window2", [P, TOKENS], F32, tag="k_il1"))
-        windows.append(sbuf("window3", [P, TOKENS], F32, tag="z_turned0"))
-        for j in range(2, 4):
+        windows = []
+        for j, tag in enumerate(("k_il1", "z_turned0", "z_turned1", "z_turned2")):
+            windows.append(sbuf("window%d" % j, [P, TOKENS], F32, tag=tag))
             nc.gpsimd.memset(windows[j][:], 0.0)
 
-        v_turned = [bank(b, "v0_turned%d" % b, [P, PACK, P]) for b in range(PACK)]
         e_all, u_all, ce_all = [], [], []
 
         def turn_and_add(banks, l, t):
@@ -170,45 +174,72 @@ def tile_attend_gjoint_kk_kernel(tc, qT, kT, dp, dq, us, ts, wt, offs, woffs, ou
                 nc.tensor.matmul(banks[b][:, t, :], ce_all[t][:, l, blk(b)], ident[:], start=False, stop=True,
                                  is_transpose=True)
 
-        def centre(l, t):
-            nc.scalar.activation(ce_all[t][:, l, :], e_all[t][:, l, :], ACT.Copy, scale=stat[t][:, 6:7])
+        def scaled_copy(on_vector, dst, src, scale):
+            if on_vector:
+                nc.vector.tensor_scalar(dst, src, scale, None, ALU.mult)
+            else:
+                nc.scalar.activation(dst, src, ACT.Copy, scale=scale)
 
-        for t in range(PACK):
+        def centre(l, t):
+            if l == 0 and t == PACK - 1:
+                nc.vector.tensor_scalar(ce_all[t][:, l, :], e_all[t][:, l, :], normed[:, t, 1:2], stat[t][:, 5:6],
+                                        ALU.mult, ALU.mult)
+            else:
+                nc.scalar.activation(ce_all[t][:, l, :], e_all[t][:, l, :], ACT.Copy, scale=stat[t][:, 6:7])
+
+        def turn_back(l, u, banks, backs):
+            for b in range(PACK):
+                g_t = sbuf("g_turned%d_%d_%d" % (l, b, u), [P, P, 2], BF16)
+                src = banks[b][:, 2 * u:2 * u + 2, :].rearrange("n e s -> n s e")
+                scaled_copy(l == 0 and u == 1 and b >= 2, g_t[:], src, ts_col[l][:, b:b + 1])
+                words = g_t[:].rearrange("n s e -> n (s e)").bitcast(F32)
+                nc.tensor.transpose(backs[b // 2][:, b % 2, u, :], words, ident[:])
+
+        total = sbuf("total", [P, PACK], F32)
+        inv = sbuf("inv", [P, PACK], F32)
+        normed = sbuf("normed", [P, PACK, 2], F32)
+
+        def weights(t):
             st = stat[t]
             nc.vector.tensor_scalar(neg_z[t][:, 0, :], z_back[t][:], neg_us[:, t:t + 1], st[:, 0:1], ALU.mult, ALU.min,
                                     accum_out=st[:, 1:2])
             e = sbuf("e%d" % t, [P, 2, SLOTS], F32)
-            nc.scalar.activation(e[:], neg_z[t][:], ACT.Exp, bias=st[:, 1:2], scale=-1.0, accum_out=st[:, 2:3])
-            nc.vector.reciprocal(st[:, 3:4], st[:, 2:3])
-            nc.vector.tensor_scalar(st[:, 4:5], st[:, 3:4], wt_us[:, t:t + 1], None, ALU.mult)
-            u = sbuf("u%d" % t, [P, 2, SLOTS], F32, tag="k_plane%d" % t)
-            nc.vector.scalar_tensor_tensor(u[:], e[:], st[:, 4:5], dpq[:, :, t, :], ALU.mult, ALU.mult,
-                                           accum_out=st[:, 5:6])
-            nc.vector.tensor_scalar(st[:, 6:7], st[:, 5:6], st[:, 3:4], -1.0, ALU.mult, ALU.mult)
-            ce = sbuf("ce%d" % t, [P, 2, SLOTS], F32, tag="neg_z%d" % t)
+            nc.scalar.activation(e[:], neg_z[t][:], ACT.Exp, bias=st[:, 1:2], scale=-1.0, accum_out=total[:, t:t + 1])
             e_all.append(e)
+
+        for t in range(PACK - 1):
+            weights(t)
+        v_turned = [bank(b, "v0_turned%d" % b, [P, PACK, P]) for b in range(PACK)]
+        g_back = [bank(4 + h, "g_back0_%d" % h, [P, 2, 2, P]) for h in range(2)]
+        for t in range(PACK):
+            st, e = stat[t], e_all[t]
+            if t % 2 == 0:
+                pair = slice(t, t + 2)
+                nc.vector.reciprocal(inv[:, pair], total[:, pair])
+                nc.vector.tensor_tensor(normed[:, pair, :], inv[:, pair].unsqueeze(2).to_broadcast([P, 2, 2]),
+                                        factors[:, pair, :], ALU.mult)
+            u = sbuf("u%d" % t, [P, 2, SLOTS], F32, tag="k_plane%d" % t)
+            nc.vector.scalar_tensor_tensor(u[:], e[:], normed[:, t, 0:1], dpq[:, :, t, :], ALU.mult, ALU.mult,
+                                           accum_out=st[:, 5:6])
+            nc.scalar.activation(st[:, 6:7], st[:, 5:6], ACT.Copy, scale=normed[:, t, 1:2])
+            ce = sbuf("ce%d" % t, [P, 2, SLOTS], F32, tag="neg_z%d" % t)
+            if t == 0:
+                weights(PACK - 1)
             u_all.append(u)
             ce_all.append(ce)
             centre(0, t)
             turn_and_add(v_turned, 0, t)
+            if t == PACK - 1:
+                q_r = quantise("q_r", q2_il[:].rearrange("s j m t -> s (j m t)"), E4M3, tag="dpq")
+            if t % 2 == 1:
+                turn_back(0, t // 2, v_turned, g_back)
 
-        def finish(l, banks):
+        def finish(l, backs):
             g_il = sbuf("g_il%d" % l, [P, SLOTS, PACK], BF16)
             g_words = g_il[:].rearrange("s c t -> s (c t)").bitcast(F32).rearrange("s (b n u) -> s b n u", b=PACK, u=2)
             for h in range(2):
                 on_vector = l == 0 and h == 1
-                back = bank(4 + h, "g_back%d_%d" % (l, h), [P, 2, 2, P])
-                for bb in range(2):
-                    b = 2 * h + bb
-                    g_t = sbuf("g_turned%d_%d" % (l, b), [P, 2, P, 2], BF16)
-                    src = banks[b][:].rearrange("n (u e) s -> n u s e", e=2)
-                    if on_vector:
-                        nc.vector.tensor_scalar(g_t[:], src, ts_col[l][:, b:b + 1], None, ALU.mult)
-                    else:
-                        nc.scalar.activation(g_t[:], src, ACT.Copy, scale=ts_col[l][:, b:b + 1])
-                    words = g_t[:].rearrange("n u s e -> n (u s e)").bitcast(F32)
-                    for u in range(2):
-                        nc.tensor.transpose(back[:, bb, u, :], words[:, blk(u)], ident[:])
+                back = backs[h]
                 src = back[:].rearrange("s b u n -> s b n u")
                 if on_vector:
                     nc.vector.tensor_copy(g_words[:, 2 * h:2 * h + 2], src)
@@ -218,22 +249,34 @@ def tile_attend_gjoint_kk_kernel(tc, qT, kT, dp, dq, us, ts, wt, offs, woffs, ou
 
         out_rows = out.rearrange("(m j) c -> m j c", j=PACK)
 
-        def place(l, j, g_q, tag=None):
-            acc = bank(6 + j % 2, "d%d_%d" % (l, j), [P, SLOTS])
+        def place(l, j, g_q, bank_no):
+            acc = bank(bank_no, "d%d_%d" % (l, j), [P, SLOTS])
             mx(acc[:], q_r, blk(j), g_q, E5M2)
-            d_sb = sbuf("d_sb%d_%d" % (l, j), [P, SLOTS], F32, tag=tag)
-            nc.scalar.copy(d_sb[:], acc[:])
-            nc.vector.tensor_copy(windows[j][:].indirect(lists[l][:]), d_sb[:])
+            d_sb = sbuf("d_sb%d_%d" % (l, j), [P, SLOTS], F32)
+            pieces = 2 if (l, j) == (0, 0) else 1
+            width = SLOTS // pieces
+            for h in range(pieces):
+                cols = slice(h * width, (h + 1) * width)
+                nc.scalar.copy(d_sb[:, cols], acc[:, cols])
+                nc.vector.tensor_copy(windows[j][:].indirect(lists[l][:, h * width // 16:(h + 1) * width // 16]),
+                                      d_sb[:, cols])
 
-        g_q0 = finish(0, v_turned)
+        g_q0 = finish(0, g_back)
         for j in range(PACK - 1):
-            place(0, j, g_q0)
+            place(0, j, g_q0, 6 + j % 2)
         v_turned = [bank(b, "v1_turned%d" % b, [P, PACK, P]) for b in range(PACK)]
+        g_back = [bank(4 + h, "g_back1_%d" % h, [P, 2, 2, P]) for h in range(2)]
         for t in range(PACK):
             centre(1, t)
             turn_and_add(v_turned, 1, t)
-        g_q1 = finish(1, v_turned)
-        place(0, PACK - 1, g_q0, tag="g_il1")
+            if t % 2 == 1:
+                turn_back(1, t // 2, v_turned, g_back)
+        g_q1 = finish(1, g_back)
+        place(0, PACK - 1, g_q0, 5)
         for j in range(PACK):
-            place(1, j, g_q1)
-            nc.sync.dma_start(out_rows[:, j, :], windows[j][:])
+            place(1, j, g_q1, 6 + j % 2)
+            if j < PACK - 1:
+                nc.sync.dma_start(out_rows[:, j, :], windows[j][:])
+            else:
+                nc.sync.dma_start(out_rows[:, j, 0:TOKENS // 2], windows[j][:, 0:TOKENS // 2])
+                nc.scalar.dma_start(out_rows[:, j, TOKENS // 2:], windows[j][:, TOKENS // 2:])

@@ -21,6 +21,7 @@ R = 512
 SLOTS = 512
 TOKENS = 2048
 Q_SPLIT = 80
+HALF = SLOTS // 2
 FLOPS = 4 * 2 * D * R * SLOTS
 
 
@@ -42,9 +43,9 @@ def tile_attend_gjoint_kk_kernel(tc, qT, kT, dp, dq, us, ts, wt, offs, woffs, ou
             nc.vector.quantize_mx(out=codes[:].bitcast(fmt), scales=scales[:], in_=src)
             return codes, scales
 
-        def mx(dst, lhs, cols, rhs, rhs_fmt):
+        def mx(dst, lhs, cols, rhs):
             nc.tensor.matmul_mx(out=dst, lhsT=lhs[0][:, cols].bitcast(E4M3), lhsT_scale=lhs[1][:, cols],
-                                rhs=rhs[0][:].bitcast(rhs_fmt), rhs_scale=rhs[1][:], start=True, stop=True)
+                                rhs=rhs[0][:].bitcast(E4M3), rhs_scale=rhs[1][:], start=True, stop=True)
 
         def blk(b):
             return slice(b * P, (b + 1) * P)
@@ -71,12 +72,17 @@ def tile_attend_gjoint_kk_kernel(tc, qT, kT, dp, dq, us, ts, wt, offs, woffs, ou
                 rows = slice(2 * half, 2 * half + 2)
                 nc.sync.dma_start(dpq[:, l, rows, :], grad.rearrange("(p t) c -> p t c", t=PACK)[:, rows, :])
 
-        nc.gpsimd.memset(ts_win[0:P - 1, :], 0.0)
+        nc.vector.memset(ts_win[0:P - 1, :], 0.0)
         ident = sbuf("ident", [P, P], F32)
         make_identity(nc, ident[:])
         ident_bf = sbuf("ident_bf", [P, P], BF16)
         make_identity(nc, ident_bf[:])
 
+
+        g0_codes = sbuf("g0_codes", [P, HALF + SLOTS], U32)
+        g0_scales = sbuf("g0_scales", [P, HALF + SLOTS], U8)
+        nc.vector.memset(g0_codes[:, :HALF], 0)
+        nc.vector.memset(g0_scales[:, :HALF].bitcast(U32), 0)
 
         ts_g = sbuf("ts_g", [P, 2, SLOTS], F32)
         ts_col = []
@@ -93,6 +99,12 @@ def tile_attend_gjoint_kk_kernel(tc, qT, kT, dp, dq, us, ts, wt, offs, woffs, ou
             nc.tensor.transpose(spread[:, blk(b)], ts_col[1][:, b:b + 1].to_broadcast([P, P]), ident[:])
         ts_row = sbuf("ts_row", [P, SLOTS], F32)
         nc.scalar.copy(ts_row[:], spread[:])
+
+        spread = bank(3, "ts_spread_half", [P, HALF])
+        for b in range(2):
+            nc.tensor.transpose(spread[:, blk(b)], ts_col[0][:, b:b + 1].to_broadcast([P, P]), ident[:])
+        ts_half = sbuf("ts_half", [P, HALF], F32)
+        nc.scalar.copy(ts_half[:], spread[:])
 
         k_g = [sbuf("k_g%d" % l, [P, PACK, SLOTS], BF16) for l in range(2)]
 
@@ -139,7 +151,7 @@ def tile_attend_gjoint_kk_kernel(tc, qT, kT, dp, dq, us, ts, wt, offs, woffs, ou
         z_turned = []
         for b in range(PACK):
             acc = bank(b % 2, "a_turned%d" % b, [P, R])
-            mx(acc[:], k_q[0], blk(b), q_d, E4M3)
+            mx(acc[:], k_q[0], blk(b), q_d)
             zt = sbuf("z_turned%d" % b, [P, R], F32)
             nc.scalar.activation(zt[:], acc[:], ACT.Copy, scale=ts_col[0][:, b:b + 1])
             z_turned.append(zt)
@@ -148,7 +160,7 @@ def tile_attend_gjoint_kk_kernel(tc, qT, kT, dp, dq, us, ts, wt, offs, woffs, ou
 
         def window_scores(t):
             acc = bank(2 + t % 2, "b%d" % t, [P, SLOTS])
-            mx(acc[:], q_d, blk(t), k_q[1], E4M3)
+            mx(acc[:], q_d, blk(t), k_q[1])
             nc.vector.scalar_tensor_tensor(neg_z[t][:, 1, :], acc[:], neg_us[:, t:t + 1], ts_row[:], ALU.mult, ALU.mult)
             nc.vector.tensor_reduce(stat[t][:, 0:1], neg_z[t][:, 1, :], AXIS.X, ALU.min)
 
@@ -160,19 +172,18 @@ def tile_attend_gjoint_kk_kernel(tc, qT, kT, dp, dq, us, ts, wt, offs, woffs, ou
                 nc.tensor.transpose(z_back[t][:, blk(b)], z_turned[b][:, blk(t)], ident[:])
 
         windows = []
-        for j, tag in enumerate(("k_il1", "z_turned0", "z_turned1", "z_turned2")):
+        for j, tag in enumerate(("k_q0_codes", "z_turned0", "z_turned1", "z_turned2")):
             windows.append(sbuf("window%d" % j, [P, TOKENS], F32, tag=tag))
             nc.gpsimd.memset(windows[j][:], 0.0)
 
         e_all, u_all, ce_all = [], [], []
 
-        def turn_and_add(banks, l, t):
-            for b in range(PACK):
-                nc.tensor.matmul(banks[b][:, t, :], u_all[t][:, l, blk(b)], ident[:], start=True, stop=False,
-                                 is_transpose=True)
-            for b in range(PACK):
-                nc.tensor.matmul(banks[b][:, t, :], ce_all[t][:, l, blk(b)], ident[:], start=False, stop=True,
-                                 is_transpose=True)
+        def turn_and_add(banks, l, t, halves=(0, 1)):
+            for h in halves:
+                for term, first in ((u_all, True), (ce_all, False)):
+                    for b in (2 * h, 2 * h + 1):
+                        nc.tensor.matmul(banks[b][:, t, :], term[t][:, l, blk(b)], ident[:], start=first,
+                                         stop=not first, is_transpose=True)
 
         def scaled_copy(on_vector, dst, src, scale):
             if on_vector:
@@ -180,20 +191,15 @@ def tile_attend_gjoint_kk_kernel(tc, qT, kT, dp, dq, us, ts, wt, offs, woffs, ou
             else:
                 nc.scalar.activation(dst, src, ACT.Copy, scale=scale)
 
-        def centre(l, t):
-            if l == 0 and t == PACK - 1:
-                nc.vector.tensor_scalar(ce_all[t][:, l, :], e_all[t][:, l, :], normed[:, t, 1:2], stat[t][:, 5:6],
-                                        ALU.mult, ALU.mult)
-            else:
-                nc.scalar.activation(ce_all[t][:, l, :], e_all[t][:, l, :], ACT.Copy, scale=stat[t][:, 6:7])
+        def centre(l, t, cols=slice(0, SLOTS)):
+            nc.scalar.activation(ce_all[t][:, l, cols], e_all[t][:, l, cols], ACT.Copy, scale=stat[t][:, 6:7])
 
-        def turn_back(l, u, banks, backs):
-            for b in range(PACK):
-                g_t = sbuf("g_turned%d_%d_%d" % (l, b, u), [P, P, 2], BF16)
-                src = banks[b][:, 2 * u:2 * u + 2, :].rearrange("n e s -> n s e")
-                scaled_copy(l == 0 and u == 1 and b >= 2, g_t[:], src, ts_col[l][:, b:b + 1])
-                words = g_t[:].rearrange("n s e -> n (s e)").bitcast(F32)
-                nc.tensor.transpose(backs[b // 2][:, b % 2, u, :], words, ident[:])
+        def turn_back(l, u, b, banks, backs, on_vector=False):
+            g_t = sbuf("g_turned%d_%d_%d" % (l, b, u), [P, P, 2], BF16)
+            src = banks[b][:, 2 * u:2 * u + 2, :].rearrange("n e s -> n s e")
+            scaled_copy(on_vector, g_t[:], src, ts_col[l][:, b:b + 1])
+            words = g_t[:].rearrange("n s e -> n (s e)").bitcast(F32)
+            nc.tensor.transpose(backs[b][u], words, ident[:])
 
         total = sbuf("total", [P, PACK], F32)
         inv = sbuf("inv", [P, PACK], F32)
@@ -210,71 +216,111 @@ def tile_attend_gjoint_kk_kernel(tc, qT, kT, dp, dq, us, ts, wt, offs, woffs, ou
         for t in range(PACK - 1):
             weights(t)
         v_turned = [bank(b, "v0_turned%d" % b, [P, PACK, P]) for b in range(PACK)]
-        g_back = [bank(4 + h, "g_back0_%d" % h, [P, 2, 2, P]) for h in range(2)]
+        early = bank(4, "g_back0_early", [P, 2, P])
+        late = [bank(6 + bb, "g_back0_late%d" % bb, [P, 2, P]) for bb in range(2)]
+        g_back = [[early[:, 0, :]], [early[:, 1, :]]] + [[late[bb][:, u, :] for u in range(2)] for bb in range(2)]
+        g_il = [sbuf("g_il0_%d" % h, [P, HALF * PACK], BF16) for h in range(2)]
+
+        def as_words(tile):
+            return tile[:].bitcast(F32).rearrange("s (b n u) -> s b n u", n=P, u=2)
+
         for t in range(PACK):
             st, e = stat[t], e_all[t]
-            if t % 2 == 0:
-                pair = slice(t, t + 2)
-                nc.vector.reciprocal(inv[:, pair], total[:, pair])
-                nc.vector.tensor_tensor(normed[:, pair, :], inv[:, pair].unsqueeze(2).to_broadcast([P, 2, 2]),
-                                        factors[:, pair, :], ALU.mult)
+            if t != 2:
+                n = 2 if t == 1 else 1
+                group = slice(t, t + n)
+                nc.vector.reciprocal(inv[:, group], total[:, group])
+                nc.vector.tensor_tensor(normed[:, group, :], inv[:, group].unsqueeze(2).to_broadcast([P, n, 2]),
+                                        factors[:, group, :], ALU.mult)
             u = sbuf("u%d" % t, [P, 2, SLOTS], F32, tag="k_plane%d" % t)
             nc.vector.scalar_tensor_tensor(u[:], e[:], normed[:, t, 0:1], dpq[:, :, t, :], ALU.mult, ALU.mult,
                                            accum_out=st[:, 5:6])
-            nc.scalar.activation(st[:, 6:7], st[:, 5:6], ACT.Copy, scale=normed[:, t, 1:2])
+            scaled_copy(t == PACK - 1, st[:, 6:7], st[:, 5:6], normed[:, t, 1:2])
             ce = sbuf("ce%d" % t, [P, 2, SLOTS], F32, tag="neg_z%d" % t)
             if t == 0:
                 weights(PACK - 1)
             u_all.append(u)
             ce_all.append(ce)
-            centre(0, t)
-            turn_and_add(v_turned, 0, t)
-            if t == PACK - 1:
-                q_r = quantise("q_r", q2_il[:].rearrange("s j m t -> s (j m t)"), E4M3, tag="dpq")
-            if t % 2 == 1:
-                turn_back(0, t // 2, v_turned, g_back)
+            if t < 2:
+                centre(0, t)
+                turn_and_add(v_turned, 0, t)
+            if t == 1:
+                for b in range(PACK):
+                    turn_back(0, 0, b, v_turned, g_back)
+                nc.scalar.copy(as_words(g_il[0])[:, :, :, 0], early[:])
+            if t == 2:
+                centre(0, t, slice(HALF, SLOTS))
+                turn_and_add(v_turned, 0, t, halves=(1,))
 
-        def finish(l, backs):
-            g_il = sbuf("g_il%d" % l, [P, SLOTS, PACK], BF16)
-            g_words = g_il[:].rearrange("s c t -> s (c t)").bitcast(F32).rearrange("s (b n u) -> s b n u", b=PACK, u=2)
-            for h in range(2):
-                on_vector = l == 0 and h == 1
-                back = backs[h]
-                src = back[:].rearrange("s b u n -> s b n u")
-                if on_vector:
-                    nc.vector.tensor_copy(g_words[:, 2 * h:2 * h + 2], src)
-                else:
-                    nc.scalar.copy(g_words[:, 2 * h:2 * h + 2], src)
-            return quantise("g_q%d" % l, g_il[:].rearrange("s c t -> s (c t)"), E5M2)
+        q_r = (sbuf("q_r_codes", [P, D], U32, tag="dpq"), sbuf("q_r_scales", [P, D], U8))
+
+        def quantise_q_r(cols):
+            nc.vector.quantize_mx(out=q_r[0][:, cols].bitcast(E4M3), scales=q_r[1][:, cols],
+                                  in_=q2_il[:].rearrange("s j m t -> s (j m t)")[:, PACK * cols.start:PACK * cols.stop])
+
+        g_late = sbuf("g_late", [P, 2, HALF], BF16)
+        diff = sbuf("diff", [P, 2, HALF], F32)
+        for t in (2, 3):
+            nc.vector.scalar_tensor_tensor(diff[:, t - 2, :], e_all[t][:, 0, :HALF], stat[t][:, 6:7],
+                                           u_all[t][:, 0, :HALF], ALU.mult, ALU.add)
+        nc.vector.tensor_tensor(g_late[:], diff[:], ts_half[:].unsqueeze(1).to_broadcast([P, 2, HALF]), ALU.mult)
+        quantise_q_r(slice(0, P))
+        nc.vector.tensor_copy(g_il[0][:].rearrange("s (c u e) -> s c u e", u=2, e=2)[:, :, 1, :],
+                              g_late[:].rearrange("s e c -> s c e"))
+
+        def move_words(on_vector, dst, src):
+            if on_vector:
+                nc.vector.tensor_copy(dst, src)
+            else:
+                nc.scalar.copy(dst, src)
 
         out_rows = out.rearrange("(m j) c -> m j c", j=PACK)
 
-        def place(l, j, g_q, bank_no):
-            acc = bank(bank_no, "d%d_%d" % (l, j), [P, SLOTS])
-            mx(acc[:], q_r, blk(j), g_q, E5M2)
-            d_sb = sbuf("d_sb%d_%d" % (l, j), [P, SLOTS], F32)
-            pieces = 2 if (l, j) == (0, 0) else 1
-            width = SLOTS // pieces
-            for h in range(pieces):
-                cols = slice(h * width, (h + 1) * width)
-                nc.scalar.copy(d_sb[:, cols], acc[:, cols])
-                nc.vector.tensor_copy(windows[j][:].indirect(lists[l][:, h * width // 16:(h + 1) * width // 16]),
-                                      d_sb[:, cols])
+        def place(l, j, g_q, bank_no, live=slice(0, SLOTS), first=0):
+            acc = bank(bank_no, "d%d_%d_%d" % (l, j, first), [P, SLOTS])
+            nc.tensor.matmul_mx(out=acc[:], lhsT=q_r[0][:, blk(j)].bitcast(E4M3), lhsT_scale=q_r[1][:, blk(j)],
+                                rhs=g_q[0].bitcast(E5M2), rhs_scale=g_q[1], start=True, stop=True)
+            width = live.stop - live.start
+            d_sb = sbuf("d_sb%d_%d_%d" % (l, j, first), [P, width], F32)
+            nc.scalar.copy(d_sb[:], acc[:, live])
+            nc.vector.tensor_copy(windows[j][:].indirect(lists[l][:, first // 16:(first + width) // 16]), d_sb[:])
 
-        g_q0 = finish(0, g_back)
-        for j in range(PACK - 1):
-            place(0, j, g_q0, 6 + j % 2)
+        def first_product(h):
+            cols = slice((h + 1) * HALF, (h + 2) * HALF)
+            nc.vector.quantize_mx(out=g0_codes[:, cols].bitcast(E5M2), scales=g0_scales[:, cols], in_=g_il[h][:])
+            cols = slice(h * HALF, (h + 2) * HALF)
+            place(0, 0, (g0_codes[:, cols], g0_scales[:, cols]), 5 - h, live=slice(HALF, SLOTS), first=h * HALF)
+
+        first_product(0)
+        centre(0, 3, slice(HALF, SLOTS))
+        turn_and_add(v_turned, 0, 3, halves=(1,))
+        quantise_q_r(slice(P, 2 * P))
+        quantise_q_r(slice(2 * P, D))
+        for bb in range(2):
+            turn_back(0, 1, 2 + bb, v_turned, g_back)
+        for bb in range(2):
+            move_words(bb == 1, as_words(g_il[1])[:, bb], late[bb][:].rearrange("s u n -> s n u"))
+        first_product(1)
+        g_q0 = (g0_codes[:, HALF:], g0_scales[:, HALF:])
+        for j in range(1, PACK - 1):
+            place(0, j, g_q0, 5 + j)
+
         v_turned = [bank(b, "v1_turned%d" % b, [P, PACK, P]) for b in range(PACK)]
-        g_back = [bank(4 + h, "g_back1_%d" % h, [P, 2, 2, P]) for h in range(2)]
+        g_pairs = [bank(4 + h, "g_back1_%d" % h, [P, 2, 2, P]) for h in range(2)]
+        g_back = [[g_pairs[b // 2][:, b % 2, u, :] for u in range(2)] for b in range(PACK)]
         for t in range(PACK):
             centre(1, t)
             turn_and_add(v_turned, 1, t)
             if t % 2 == 1:
-                turn_back(1, t // 2, v_turned, g_back)
-        g_q1 = finish(1, g_back)
+                for b in range(PACK):
+                    turn_back(1, t // 2, b, v_turned, g_back)
+        g_il = sbuf("g_il1", [P, SLOTS * PACK], BF16)
+        for h in range(2):
+            nc.scalar.copy(as_words(g_il)[:, 2 * h:2 * h + 2], g_pairs[h][:].rearrange("s b u n -> s b n u"))
+        codes, scales = quantise("g_q1", g_il[:], E5M2)
         place(0, PACK - 1, g_q0, 5)
         for j in range(PACK):
-            place(1, j, g_q1, 6 + j % 2)
+            place(1, j, (codes[:], scales[:]), 6 + j % 2)
             if j < PACK - 1:
                 nc.sync.dma_start(out_rows[:, j, :], windows[j][:])
             else:

from contextlib import ExitStack

import concourse.mybir as mybir
from concourse.masks import make_identity

F32 = mybir.dt.float32
BF16 = mybir.dt.bfloat16
U32 = mybir.dt.uint32
U16 = mybir.dt.uint16
U8 = mybir.dt.uint8
E4M3 = mybir.dt.float8_e4m3fn_x4
E5M2 = mybir.dt.float8_e5m2_x4
ALU = mybir.AluOpType
ACT = mybir.ActivationFunctionType
AXIS = mybir.AxisListType

P = 128
PACK = 4
D = 512
R = 512
SLOTS = 512
TOKENS = 2048
Q_SPLIT = 80
HALF = SLOTS // 2
FLOPS = 4 * 2 * D * R * SLOTS


def tile_attend_gjoint_kk_kernel(tc, qT, kT, dp, dq, us, ts, wt, offs, woffs, out):
    nc = tc.nc
    with ExitStack() as ctx:
        sb = ctx.enter_context(tc.tile_pool(name="sb", bufs=1))
        ps = ctx.enter_context(tc.psum_pool(name="ps", bufs=1))

        def sbuf(name, shape, dtype, tag=None):
            return sb.tile(shape, dtype, name=name, tag=tag or name, align_bytes=64)

        def bank(n, name, shape, dtype=F32):
            return ps.tile(shape, dtype, name=name, tag="bank%d" % n)

        def quantise(name, src, fmt, tag=None):
            codes = sbuf(name + "_codes", [P, 512], U32, tag=tag)
            scales = sbuf(name + "_scales", [P, 512], U8)
            nc.vector.quantize_mx(out=codes[:].bitcast(fmt), scales=scales[:], in_=src)
            return codes, scales

        def mx(dst, lhs, cols, rhs):
            nc.tensor.matmul_mx(out=dst, lhsT=lhs[0][:, cols].bitcast(E4M3), lhsT_scale=lhs[1][:, cols],
                                rhs=rhs[0][:].bitcast(E4M3), rhs_scale=rhs[1][:], start=True, stop=True)

        def blk(b):
            return slice(b * P, (b + 1) * P)

        lists = [sbuf("offs_sb", [P, SLOTS // 16], U16), sbuf("woffs_sb", [P, SLOTS // 16], U16)]
        nc.sync.dma_start(lists[0][:], offs)
        nc.sync.dma_start(lists[1][:], woffs)
        ts_win = sbuf("ts_win", [P, TOKENS], F32)
        nc.sync.dma_start(ts_win[P - 1:P, :], ts[P - 1:P, :])
        k_rows = kT.rearrange("(p j) c -> p j c", j=PACK)
        planes = [sbuf("k_plane%d" % j, [P, TOKENS], F32) for j in range(PACK)]
        q_raw = sbuf("q_raw", [P, PACK, R], F32)
        nc.sync.dma_start(planes[0][:], k_rows[:, 0, :])
        nc.sync.dma_start(q_raw[:], qT.rearrange("(p j) r -> p j r", j=PACK))
        for j in range(1, PACK):
            nc.sync.dma_start(planes[j][:], k_rows[:, j, :])
        us_sb = sbuf("us_sb", [P, PACK], F32)
        wt_sb = sbuf("wt_sb", [P, PACK], F32)
        nc.sync.dma_start(us_sb[:], us.rearrange("(p t) o -> p (t o)", t=PACK))
        nc.sync.dma_start(wt_sb[:], wt.rearrange("(p t) o -> p (t o)", t=PACK))
        dpq = sbuf("dpq", [P, 2, PACK, SLOTS], F32)
        for half in range(2):
            for l, grad in enumerate((dp, dq)):
                rows = slice(2 * half, 2 * half + 2)
                nc.sync.dma_start(dpq[:, l, rows, :], grad.rearrange("(p t) c -> p t c", t=PACK)[:, rows, :])

        nc.vector.memset(ts_win[0:P - 1, :], 0.0)
        ident = sbuf("ident", [P, P], F32)
        make_identity(nc, ident[:])
        ident_bf = sbuf("ident_bf", [P, P], BF16)
        make_identity(nc, ident_bf[:])


        g0_codes = sbuf("g0_codes", [P, HALF + SLOTS], U32)
        g0_scales = sbuf("g0_scales", [P, HALF + SLOTS], U8)
        nc.vector.memset(g0_codes[:, :HALF], 0)
        nc.vector.memset(g0_scales[:, :HALF].bitcast(U32), 0)

        ts_g = sbuf("ts_g", [P, 2, SLOTS], F32)
        ts_col = []
        for l in range(2):
            nc.vector.tensor_copy(ts_g[:, l, :], ts_win[:].indirect(lists[l][:]))
            turned = bank(l, "ts_turned%d" % l, [P, PACK, P])
            for b in range(PACK):
                nc.tensor.transpose(turned[:, b, :], ts_g[:, l, blk(b)], ident[:])
            col = sbuf("ts_col%d" % l, [P, PACK], F32)
            nc.scalar.activation(col[:], turned[:, :, P - 1], ACT.Copy)
            ts_col.append(col)
        spread = bank(2, "ts_spread", [P, SLOTS])
        for b in range(PACK):
            nc.tensor.transpose(spread[:, blk(b)], ts_col[1][:, b:b + 1].to_broadcast([P, P]), ident[:])
        ts_row = sbuf("ts_row", [P, SLOTS], F32)
        nc.scalar.copy(ts_row[:], spread[:])

        spread = bank(3, "ts_spread_half", [P, HALF])
        for b in range(2):
            nc.tensor.transpose(spread[:, blk(b)], ts_col[0][:, b:b + 1].to_broadcast([P, P]), ident[:])
        ts_half = sbuf("ts_half", [P, HALF], F32)
        nc.scalar.copy(ts_half[:], spread[:])

        k_g = [sbuf("k_g%d" % l, [P, PACK, SLOTS], BF16) for l in range(2)]

        def gather_plane(j):
            for l in range(2):
                nc.vector.tensor_copy(k_g[l][:, j, :], planes[j][:].indirect(lists[l][:]))

        gather_plane(0)

        q_il = sbuf("q_il", [P, PACK, P, PACK], BF16)
        dst = q_il[:].rearrange("p t s j -> p s t j")
        src = q_raw[:].rearrange("p j (s t) -> p s t j", t=PACK)
        nc.vector.tensor_copy(dst[:, :Q_SPLIT], src[:, :Q_SPLIT])
        nc.scalar.copy(dst[:, Q_SPLIT:], src[:, Q_SPLIT:])
        q_d = quantise("q_d", q_il[:].rearrange("p t s j -> p (t s j)"), E4M3)

        for j in range(1, PACK):
            gather_plane(j)

        q2_il = sbuf("q2_il", [P, PACK, P, PACK], BF16)
        for j in range(PACK):
            turned = bank(4 + j, "q_turned%d" % j, [P, PACK, P], BF16)
            for t in range(PACK):
                nc.tensor.transpose(turned[:, t, :], q_il[:, t, :, j], ident_bf[:])
            nc.scalar.copy(q2_il[:, j, :, :], turned[:].rearrange("s t m -> s m t"))

        neg_us = sbuf("neg_us", [P, PACK], F32)
        nc.vector.tensor_scalar(neg_us[:], us_sb[:], -1.0, None, ALU.mult)
        factors = sbuf("factors", [P, PACK, 2], F32)
        nc.vector.memset(factors[:, :, 1], -1.0)
        nc.vector.tensor_tensor(factors[:, :, 0], us_sb[:], wt_sb[:], ALU.mult)

        k_q = []
        for l in range(2):
            k_il = sbuf("k_il%d" % l, [P, SLOTS, PACK], BF16)
            dst = k_il[:].rearrange("p (c i) j -> p c j i", i=4)
            src = k_g[l][:].rearrange("p j (c i) -> p c j i", i=4)
            if l == 0:
                nc.scalar.copy(dst, src)
            else:
                nc.vector.tensor_copy(dst, src)
            k_q.append(quantise("k_q%d" % l, k_il[:].rearrange("p c j -> p (c j)"), E4M3))

        z_turned = []
        for b in range(PACK):
            acc = bank(b % 2, "a_turned%d" % b, [P, R])
            mx(acc[:], k_q[0], blk(b), q_d)
            zt = sbuf("z_turned%d" % b, [P, R], F32)
            nc.scalar.activation(zt[:], acc[:], ACT.Copy, scale=ts_col[0][:, b:b + 1])
            z_turned.append(zt)
        neg_z = [sbuf("neg_z%d" % t, [P, 2, SLOTS], F32) for t in range(PACK)]
        stat = [sbuf("stat%d" % t, [P, 8], F32) for t in range(PACK)]

        def window_scores(t):
            acc = bank(2 + t % 2, "b%d" % t, [P, SLOTS])
            mx(acc[:], q_d, blk(t), k_q[1])
            nc.vector.scalar_tensor_tensor(neg_z[t][:, 1, :], acc[:], neg_us[:, t:t + 1], ts_row[:], ALU.mult, ALU.mult)
            nc.vector.tensor_reduce(stat[t][:, 0:1], neg_z[t][:, 1, :], AXIS.X, ALU.min)

        for t in range(PACK):
            window_scores(t)
        z_back = [bank(4 + t, "z_back%d" % t, [P, SLOTS]) for t in range(PACK)]
        for t in range(PACK):
            for b in range(PACK):
                nc.tensor.transpose(z_back[t][:, blk(b)], z_turned[b][:, blk(t)], ident[:])

        windows = []
        for j, tag in enumerate(("k_q0_codes", "z_turned0", "z_turned1", "z_turned2")):
            windows.append(sbuf("window%d" % j, [P, TOKENS], F32, tag=tag))
            nc.gpsimd.memset(windows[j][:], 0.0)

        e_all, u_all, ce_all = [], [], []

        def turn_and_add(banks, l, t, halves=(0, 1)):
            for h in halves:
                for term, first in ((u_all, True), (ce_all, False)):
                    for b in (2 * h, 2 * h + 1):
                        nc.tensor.matmul(banks[b][:, t, :], term[t][:, l, blk(b)], ident[:], start=first,
                                         stop=not first, is_transpose=True)

        def scaled_copy(on_vector, dst, src, scale):
            if on_vector:
                nc.vector.tensor_scalar(dst, src, scale, None, ALU.mult)
            else:
                nc.scalar.activation(dst, src, ACT.Copy, scale=scale)

        def centre(l, t, cols=slice(0, SLOTS)):
            nc.scalar.activation(ce_all[t][:, l, cols], e_all[t][:, l, cols], ACT.Copy, scale=stat[t][:, 6:7])

        def turn_back(l, u, b, banks, backs, on_vector=False):
            g_t = sbuf("g_turned%d_%d_%d" % (l, b, u), [P, P, 2], BF16)
            src = banks[b][:, 2 * u:2 * u + 2, :].rearrange("n e s -> n s e")
            scaled_copy(on_vector, g_t[:], src, ts_col[l][:, b:b + 1])
            words = g_t[:].rearrange("n s e -> n (s e)").bitcast(F32)
            nc.tensor.transpose(backs[b][u], words, ident[:])

        total = sbuf("total", [P, PACK], F32)
        inv = sbuf("inv", [P, PACK], F32)
        normed = sbuf("normed", [P, PACK, 2], F32)

        def weights(t):
            st = stat[t]
            nc.vector.tensor_scalar(neg_z[t][:, 0, :], z_back[t][:], neg_us[:, t:t + 1], st[:, 0:1], ALU.mult, ALU.min,
                                    accum_out=st[:, 1:2])
            e = sbuf("e%d" % t, [P, 2, SLOTS], F32)
            nc.scalar.activation(e[:], neg_z[t][:], ACT.Exp, bias=st[:, 1:2], scale=-1.0, accum_out=total[:, t:t + 1])
            e_all.append(e)

        for t in range(PACK - 1):
            weights(t)
        v_turned = [bank(b, "v0_turned%d" % b, [P, PACK, P]) for b in range(PACK)]
        early = bank(4, "g_back0_early", [P, 2, P])
        late = [bank(6 + bb, "g_back0_late%d" % bb, [P, 2, P]) for bb in range(2)]
        g_back = [[early[:, 0, :]], [early[:, 1, :]]] + [[late[bb][:, u, :] for u in range(2)] for bb in range(2)]
        g_il = [sbuf("g_il0_%d" % h, [P, HALF * PACK], BF16) for h in range(2)]

        def as_words(tile):
            return tile[:].bitcast(F32).rearrange("s (b n u) -> s b n u", n=P, u=2)

        for t in range(PACK):
            st, e = stat[t], e_all[t]
            if t != 2:
                n = 2 if t == 1 else 1
                group = slice(t, t + n)
                nc.vector.reciprocal(inv[:, group], total[:, group])
                nc.vector.tensor_tensor(normed[:, group, :], inv[:, group].unsqueeze(2).to_broadcast([P, n, 2]),
                                        factors[:, group, :], ALU.mult)
            u = sbuf("u%d" % t, [P, 2, SLOTS], F32, tag="k_plane%d" % t)
            nc.vector.scalar_tensor_tensor(u[:], e[:], normed[:, t, 0:1], dpq[:, :, t, :], ALU.mult, ALU.mult,
                                           accum_out=st[:, 5:6])
            scaled_copy(t == PACK - 1, st[:, 6:7], st[:, 5:6], normed[:, t, 1:2])
            ce = sbuf("ce%d" % t, [P, 2, SLOTS], F32, tag="neg_z%d" % t)
            if t == 0:
                weights(PACK - 1)
            u_all.append(u)
            ce_all.append(ce)
            if t < 2:
                centre(0, t)
                turn_and_add(v_turned, 0, t)
            if t == 1:
                for b in range(PACK):
                    turn_back(0, 0, b, v_turned, g_back)
                nc.scalar.copy(as_words(g_il[0])[:, :, :, 0], early[:])
            if t == 2:
                centre(0, t, slice(HALF, SLOTS))
                turn_and_add(v_turned, 0, t, halves=(1,))

        q_r = (sbuf("q_r_codes", [P, D], U32, tag="dpq"), sbuf("q_r_scales", [P, D], U8))

        def quantise_q_r(cols):
            nc.vector.quantize_mx(out=q_r[0][:, cols].bitcast(E4M3), scales=q_r[1][:, cols],
                                  in_=q2_il[:].rearrange("s j m t -> s (j m t)")[:, PACK * cols.start:PACK * cols.stop])

        g_late = sbuf("g_late", [P, 2, HALF], BF16)
        diff = sbuf("diff", [P, 2, HALF], F32)
        for t in (2, 3):
            nc.vector.scalar_tensor_tensor(diff[:, t - 2, :], e_all[t][:, 0, :HALF], stat[t][:, 6:7],
                                           u_all[t][:, 0, :HALF], ALU.mult, ALU.add)
        nc.vector.tensor_tensor(g_late[:], diff[:], ts_half[:].unsqueeze(1).to_broadcast([P, 2, HALF]), ALU.mult)
        quantise_q_r(slice(0, P))
        nc.vector.tensor_copy(g_il[0][:].rearrange("s (c u e) -> s c u e", u=2, e=2)[:, :, 1, :],
                              g_late[:].rearrange("s e c -> s c e"))

        def move_words(on_vector, dst, src):
            if on_vector:
                nc.vector.tensor_copy(dst, src)
            else:
                nc.scalar.copy(dst, src)

        out_rows = out.rearrange("(m j) c -> m j c", j=PACK)

        def place(l, j, g_q, bank_no, live=slice(0, SLOTS), first=0):
            acc = bank(bank_no, "d%d_%d_%d" % (l, j, first), [P, SLOTS])
            nc.tensor.matmul_mx(out=acc[:], lhsT=q_r[0][:, blk(j)].bitcast(E4M3), lhsT_scale=q_r[1][:, blk(j)],
                                rhs=g_q[0].bitcast(E5M2), rhs_scale=g_q[1], start=True, stop=True)
            width = live.stop - live.start
            d_sb = sbuf("d_sb%d_%d_%d" % (l, j, first), [P, width], F32)
            nc.scalar.copy(d_sb[:], acc[:, live])
            nc.vector.tensor_copy(windows[j][:].indirect(lists[l][:, first // 16:(first + width) // 16]), d_sb[:])

        def first_product(h):
            cols = slice((h + 1) * HALF, (h + 2) * HALF)
            nc.vector.quantize_mx(out=g0_codes[:, cols].bitcast(E5M2), scales=g0_scales[:, cols], in_=g_il[h][:])
            cols = slice(h * HALF, (h + 2) * HALF)
            place(0, 0, (g0_codes[:, cols], g0_scales[:, cols]), 5 - h, live=slice(HALF, SLOTS), first=h * HALF)

        first_product(0)
        centre(0, 3, slice(HALF, SLOTS))
        turn_and_add(v_turned, 0, 3, halves=(1,))
        quantise_q_r(slice(P, 2 * P))
        quantise_q_r(slice(2 * P, D))
        for bb in range(2):
            turn_back(0, 1, 2 + bb, v_turned, g_back)
        for bb in range(2):
            move_words(bb == 1, as_words(g_il[1])[:, bb], late[bb][:].rearrange("s u n -> s n u"))
        first_product(1)
        g_q0 = (g0_codes[:, HALF:], g0_scales[:, HALF:])
        for j in range(1, PACK - 1):
            place(0, j, g_q0, 5 + j)

        v_turned = [bank(b, "v1_turned%d" % b, [P, PACK, P]) for b in range(PACK)]
        g_pairs = [bank(4 + h, "g_back1_%d" % h, [P, 2, 2, P]) for h in range(2)]
        g_back = [[g_pairs[b // 2][:, b % 2, u, :] for u in range(2)] for b in range(PACK)]
        for t in range(PACK):
            centre(1, t)
            turn_and_add(v_turned, 1, t)
            if t % 2 == 1:
                for b in range(PACK):
                    turn_back(1, t // 2, b, v_turned, g_back)
        g_il = sbuf("g_il1", [P, SLOTS * PACK], BF16)
        for h in range(2):
            nc.scalar.copy(as_words(g_il)[:, 2 * h:2 * h + 2], g_pairs[h][:].rearrange("s b u n -> s b n u"))
        codes, scales = quantise("g_q1", g_il[:], E5M2)
        place(0, PACK - 1, g_q0, 5)
        for j in range(PACK):
            place(1, j, (codes[:], scales[:]), 6 + j % 2)
            if j < PACK - 1:
                nc.sync.dma_start(out_rows[:, j, :], windows[j][:])
            else:
                nc.sync.dma_start(out_rows[:, j, 0:TOKENS // 2], windows[j][:, 0:TOKENS // 2])
                nc.scalar.dma_start(out_rows[:, j, TOKENS // 2:], windows[j][:, TOKENS // 2:])
